import numpy as np
import ml_dtypes


def mxq(x, axis, fmt="e4m3"):
    dtype, down = {"e4m3": (ml_dtypes.float8_e4m3fn, 7), "e5m2": (ml_dtypes.float8_e5m2, 14)}[fmt]
    v = np.moveaxis(np.asarray(x, np.float32).astype(ml_dtypes.bfloat16).astype(np.float64), axis, -1)
    blocks = v.reshape(v.shape[:-1] + (-1, 32))
    amax = np.abs(blocks).max(-1, keepdims=True)
    byte = np.maximum(np.where(amax > 0, np.frexp(amax)[1] - 1 + 127, 0) - down, 1)
    scale = np.exp2(byte - 127.0)
    codes = (blocks / scale).astype(np.float32).astype(dtype).astype(np.float64)
    return np.moveaxis((codes * scale).reshape(v.shape), -1, axis)


WIDE = False


def mx_kscale(k):
    if not WIDE:
        return np.ones(k)
    levels = np.array([10, -10, 5, -5, 0])
    if k % 512:
        return np.exp2(np.random.permutation(np.resize(levels, k // 32))).repeat(32)
    a = np.empty((k // 512, 16))
    for p in range(k // 512):
        a[p, :8] = np.random.permutation(np.resize(levels, 8))
        for g in range(8):
            far = levels[np.abs(levels - a[p, g]) >= 10]
            a[p, g + 8] = far[np.random.randint(len(far))]
    return np.exp2(a.ravel()).repeat(32)


def f64(x):
    return np.asarray(x).astype(np.float64)


E2M1 = np.array([0.0, 0.5, 1.0, 1.5, 2.0, 3.0, 4.0, 6.0, -0.0, -0.5, -1.0, -1.5, -2.0, -3.0, -4.0, -6.0])


def pack_weight(w, fmt):
    k, n = w.shape
    w = f64(np.asarray(w, np.float32).astype(ml_dtypes.bfloat16)).reshape(k // 32, 32, n)
    amax = np.abs(w).max(1)
    if fmt == "e4m3":
        byte = np.frexp(amax)[1] - 1 + 127 - 7
    else:
        mant, ex = np.frexp(amax / 6.0)
        byte = np.where(mant > 0.5, ex, ex - 1) + 127
    byte = np.clip(np.where(amax > 0, byte, 1), 1, 254)
    scaled = (w * np.exp2(127.0 - byte)[:, None, :]).reshape(k, n).astype(np.float32)
    by_word = np.ascontiguousarray(scaled.reshape(k // 512, 128, 4, n).transpose(0, 1, 3, 2))
    if fmt == "e4m3":
        words = by_word.astype(ml_dtypes.float8_e4m3fn).view(np.uint8)
    else:
        c = by_word.astype(ml_dtypes.float4_e2m1fn).view(np.uint8) & 0xF
        words = (c[..., 0::2] | (c[..., 1::2] << 4)).reshape(k // 512, 128, 2 * n)
    return np.ascontiguousarray(words), np.ascontiguousarray(byte.astype(np.uint8).reshape(k // 512, 16, n))


def unpack_weight(words, scales, fmt):
    g, _, n = scales.shape
    words = np.ascontiguousarray(words).reshape(g, 128, n, -1)
    if fmt == "e4m3":
        vals = words.view(ml_dtypes.float8_e4m3fn).astype(np.float64)
    else:
        nib = np.empty((g, 128, n, 4), np.uint8)
        nib[..., 0::2] = words & 0xF
        nib[..., 1::2] = words >> 4
        vals = E2M1[nib]
    vals = vals * np.repeat(np.exp2(scales.astype(np.float64) - 127.0), 8, axis=1)[..., None]
    return vals.transpose(0, 1, 3, 2).reshape(g * 512, n)


def bf(x):
    return np.asarray(x, np.float32).astype(ml_dtypes.bfloat16)


def planes(Y):
    r, m = Y.shape
    b = f64(bf(Y)).reshape(r // 32, 32, m)
    amax = np.abs(b).max(1)
    byte = np.clip(np.where(amax > 0, np.frexp(amax)[1] - 1 + 127 - 7, 1), 1, 254)
    codes = (b * np.exp2(127.0 - byte)[:, None, :]).reshape(r, m).astype(np.float32).astype(ml_dtypes.float8_e4m3fn).view(np.uint8)
    words = codes.reshape(r // 512, 128, 4, m).transpose(0, 1, 3, 2)
    return np.ascontiguousarray(words), np.ascontiguousarray(byte.astype(np.uint8).reshape(r // 512, 16, m))


K, L, T, N = 1024, 1024, 512, 512


def setup_inputs():
    n = np.random.standard_normal
    fk = mx_kscale(K)
    fl = mx_kscale(L)
    xtp = pack_weight(n((K, T)) / fk[:, None], "e2m1")
    wap = pack_weight(n((K, N)) * 1 / np.sqrt(K) * fk[:, None], "e4m3")
    wqp = pack_weight(n((L, N)) * 1 / np.sqrt(L) * fl[:, None], "e2m1")
    return {
        "xt_words": xtp[0],
        "xt_scales": xtp[1],
        "wa_words": wap[0],
        "wa_scales": wap[1],
        "xq": (n((L, T)) / fl[:, None]).astype(np.float32),
        "wq_words": wqp[0],
        "wq_scales": wqp[1],
        "wc": (n((L, N)) * 1 / np.sqrt(L) * fl[:, None]).astype(np.float32),
        "th": (np.random.uniform(0.3, 0.9, (N, 1))).astype(np.float32),
    }


def reference(xt_words, xt_scales, wa_words, wa_scales, xq, wq_words, wq_scales, wc, th):
    xtu = unpack_weight(xt_words, xt_scales, "e2m1")
    wau = unpack_weight(wa_words, wa_scales, "e4m3")
    wqu = unpack_weight(wq_words, wq_scales, "e2m1")
    xqq = mxq(f64(xq), 0, "e4m3")
    p = wau.T @ xtu + wqu.T @ xqq
    wcq = mxq(f64(wc), 0, "e4m3")
    s = wcq.T @ xqq
    y = np.maximum(p - f64(th), 0.0) - np.maximum(0.0 - p - f64(th), 0.0) + np.tanh(s)
    words, scales = planes(y)
    return y, words, scales

@@ -1,0 +1,253 @@
+from contextlib import ExitStack
+
+import concourse.mybir as mybir
+
+K, L, T, N = 1024, 1024, 512, 512
+FLOPS = 2 * (K + 2 * L) * T * N
+
+F32 = mybir.dt.float32
+BF16 = mybir.dt.bfloat16
+I32 = mybir.dt.int32
+U8 = mybir.dt.uint8
+FP8X4 = mybir.dt.float8_e4m3fn_x4
+FP4X4 = mybir.dt.float4_e2m1fn_x4
+ALU = mybir.AluOpType
+ACT = mybir.ActivationFunctionType
+
+P = 128
+PACK = 4
+PASSES = 2
+K_PASS = P * PACK
+HALF = T // 2
+XQ_ON_VECTOR = 288
+LAST_ON_VECTOR = 160
+
+
+def tile_mix_sum_shrunk_by_threshold_pl_kernel(
+    tc, xt_words, xt_scales, wa_words, wa_scales, xq, wq_words, wq_scales, wc, th, out_0, out_1, out_2
+):
+    nc = tc.nc
+
+    with ExitStack() as ctx:
+        sb = ctx.enter_context(tc.tile_pool(name="sb", bufs=1))
+        ps = ctx.enter_context(tc.psum_pool(name="ps", bufs=1))
+        ctx.enter_context(tc.manual_schedule())
+
+        def new(name, shape, dtype):
+            return sb.tile(shape, dtype, name=name, align_bytes=64)
+
+        wq_raw = new("wq_raw", [P, PASSES, 2 * N], U8)
+        wq_dealt = [new("wq_dealt%d" % g, [P, 2 * N], U8) for g in range(PASSES)]
+        wa_raw = [new("wa_raw%d" % g, [P, N], I32) for g in range(PASSES)]
+        wa_dealt = [new("wa_dealt%d" % g, [P, N], I32) for g in range(PASSES)]
+        xt_codes = [new("xt_codes%d" % g, [P, 2 * T], U8) for g in range(PASSES)]
+        wq_sc_raw = new("wq_sc_raw", [P, PASSES, N], U8)
+        wa_sc_raw = new("wa_sc_raw", [P, PASSES, N], U8)
+        wq_sc = new("wq_sc", [P, PASSES, N], U8)
+        wa_sc = new("wa_sc", [P, PASSES, N], U8)
+        xt_sc = new("xt_sc", [P, PASSES, T], U8)
+        xq_raw = [new("xq_raw%d" % g, [P, PACK, T], F32) for g in range(PASSES)]
+        wc_raw = [new("wc_raw%d" % g, [P, PACK, N], F32) for g in range(PASSES)]
+        xq_bf = [new("xq_bf%d" % g, [P, T * PACK], BF16) for g in range(PASSES)]
+        xq_codes = [new("xq_codes%d" % g, [P, T], I32) for g in range(PASSES)]
+        xq_sc = [new("xq_sc%d" % g, [P, T], U8) for g in range(PASSES)]
+        wc_bf = [[new("wc_bf%d%d" % (g, h), [P, 2 * P * PACK], BF16) for h in range(2)] for g in range(PASSES)]
+        wc_codes = [[new("wc_codes%d%d" % (g, h), [P, 2 * P], I32) for h in range(2)] for g in range(PASSES)]
+        wc_sc = [[new("wc_sc%d%d" % (g, h), [P, 2 * P], U8) for h in range(2)] for g in range(PASSES)]
+        th_pos = new("th_pos", [P, PACK], F32)
+        th_neg = new("th_neg", [P, PACK], F32)
+        warm_in = new("warm_in", [P, 1], F32)
+        warm_out = new("warm_out", [P, 1], F32)
+        tanh_s = [new("tanh_s%d" % r, [P, T], F32) for r in range(PACK)]
+        upper = [[new("upper%d%d" % (r, h), [P, HALF], F32) for h in range(2)] for r in range(PACK)]
+        y = [new("y%d" % h, [P, PACK, HALF], F32) for h in range(2)]
+        y_bf = [new("y_bf%d" % h, [P, HALF * PACK], BF16) for h in range(2)]
+        y_codes = [new("y_codes%d" % h, [P, HALF], I32) for h in range(2)]
+        y_sc = new("y_sc", [P, T], U8)
+        p_acc = [ps.tile([P, T], F32, name="p_acc%d" % r) for r in range(PACK)]
+        s_acc = [ps.tile([P, T], F32, name="s_acc%d" % r) for r in range(PACK)]
+
+        def load_scales(queue, plane, scales):
+            rows = scales.rearrange("g q c -> q g c")
+            for quad in range(4):
+                queue.dma_start(
+                    out=plane[32 * quad : 32 * quad + 4, :, :].bitcast(I32),
+                    in_=rows[4 * quad : 4 * quad + 4, :, :].bitcast(I32),
+                )
+
+        def load_rows(raw, src, g):
+            nc.sync.dma_start(
+                out=raw[:], in_=src[g * K_PASS : (g + 1) * K_PASS, :].rearrange("(p j) w -> p j w", j=PACK)
+            )
+
+        def interleave(copy, bf, raw, lo, hi):
+            copy(
+                out=bf[:, PACK * lo : PACK * hi].rearrange("p (c i j) -> p c j i", i=4, j=PACK),
+                in_=raw[:, :, lo:hi].rearrange("p j (c i) -> p c j i", i=4),
+            )
+
+        def round_wc(copy, g, h):
+            copy(
+                out=wc_bf[g][h][:].rearrange("p (r m j) -> p m r j", r=2, j=PACK),
+                in_=wc_raw[g][:].rearrange("p j (m r) -> p m r j", r=PACK)[:, :, 2 * h : 2 * h + 2, :],
+            )
+
+        def quantize(codes, scales, bf):
+            nc.vector.quantize_mx(out=codes.bitcast(FP8X4), scales=scales, in_=bf)
+
+        def deal_scales(dealt, raw):
+            nc.vector.tensor_copy(
+                out=dealt[:].rearrange("p g (r b i) -> p g b r i", r=PACK, i=16),
+                in_=raw[:].rearrange("p g (b i r) -> p g b r i", r=PACK, i=16),
+            )
+
+        def wq_pass(r, g, start):
+            nc.tensor.matmul_mx(
+                out=p_acc[r][:],
+                lhsT=wq_dealt[g][:, 2 * P * r : 2 * P * (r + 1)].bitcast(FP4X4),
+                lhsT_scale=wq_sc[:, g, P * r : P * (r + 1)],
+                rhs=xq_codes[g][:].bitcast(FP8X4),
+                rhs_scale=xq_sc[g][:],
+                start=start,
+                stop=False,
+            )
+
+        def wa_pass(r, g, stop):
+            nc.tensor.matmul_mx(
+                out=p_acc[r][:],
+                lhsT=wa_dealt[g][:, P * r : P * (r + 1)].bitcast(FP8X4),
+                lhsT_scale=wa_sc[:, g, P * r : P * (r + 1)],
+                rhs=xt_codes[g][:].bitcast(FP4X4),
+                rhs_scale=xt_sc[:, g, :],
+                start=False,
+                stop=stop,
+            )
+
+        def wc_pass(r, g):
+            cols = slice(P * (r % 2), P * (r % 2 + 1))
+            nc.tensor.matmul_mx(
+                out=s_acc[r][:],
+                lhsT=wc_codes[g][r // 2][:, cols].bitcast(FP8X4),
+                lhsT_scale=wc_sc[g][r // 2][:, cols],
+                rhs=xq_codes[g][:].bitcast(FP8X4),
+                rhs_scale=xq_sc[g][:],
+                start=(g == 0),
+                stop=(g == PASSES - 1),
+            )
+
+        def add_upper(r, h):
+            cols = slice(h * HALF, (h + 1) * HALF)
+            nc.vector.scalar_tensor_tensor(
+                out=upper[r][h][:], in0=p_acc[r][:, cols], scalar=th_pos[:, r : r + 1], in1=tanh_s[r][:, cols],
+                op0=ALU.max, op1=ALU.add,
+            )
+
+        def add_lower(r, h):
+            cols = slice(h * HALF, (h + 1) * HALF)
+            nc.vector.scalar_tensor_tensor(
+                out=y[h][:, r, :], in0=p_acc[r][:, cols], scalar=th_neg[:, r : r + 1], in1=upper[r][h][:],
+                op0=ALU.min, op1=ALU.add,
+            )
+
+        def store_y(h):
+            nc.sync.dma_start(
+                out=out_0.rearrange("(p r) t -> p r t", r=PACK)[:, :, h * HALF : (h + 1) * HALF], in_=y[h][:]
+            )
+
+        def store_words(h):
+            nc.sync.dma_start(
+                out=out_1[0].rearrange("p c r -> p (c r)").bitcast(I32)[:, h * HALF : (h + 1) * HALF],
+                in_=y_codes[h][:],
+            )
+
+        def deal_wa(g):
+            nc.vector.tensor_copy(
+                out=wa_dealt[g][:].rearrange("p (r b i) -> p b r i", r=PACK, i=4),
+                in_=wa_raw[g][:].rearrange("p (b i r) -> p b r i", r=PACK, i=4),
+            )
+
+        def quantize_wc(g, h):
+            quantize(wc_codes[g][h][:], wc_sc[g][h][:], wc_bf[g][h][:])
+
+        for plane in (wq_sc_raw, wa_sc_raw):
+            nc.vector.memset(plane[:].rearrange("p g c -> p (g c)").bitcast(I32), 0)
+        nc.vector.memset(warm_in[:], 0.0)
+        nc.gpsimd.memset(xt_sc[:].rearrange("p g c -> p (g c)").bitcast(I32), 0)
+        load_scales(nc.gpsimd, xt_sc, xt_scales)
+        nc.sync.dma_start(out=wq_raw[:].bitcast(I32), in_=wq_words.rearrange("g p c -> p g c").bitcast(I32))
+        load_rows(xq_raw[0], xq, 0)
+        load_scales(nc.scalar, wq_sc_raw, wq_scales)
+        nc.scalar.activation(out=warm_out[:], in_=warm_in[:], func=ACT.Tanh)
+        load_rows(wc_raw[0], wc, 0)
+        nc.sync.dma_start(out=th_pos[:], in_=th.rearrange("(p r) o -> p (r o)", r=PACK))
+        load_scales(nc.sync, wa_sc_raw, wa_scales)
+        load_rows(xq_raw[1], xq, 1)
+        load_rows(wc_raw[1], wc, 1)
+        for g in range(PASSES):
+            nc.sync.dma_start(out=wa_raw[g][:], in_=wa_words[g].rearrange("p n t -> p (n t)").bitcast(I32))
+        for g in range(PASSES):
+            nc.sync.dma_start(out=xt_codes[g][:].bitcast(I32), in_=xt_words[g].bitcast(I32))
+
+        for g in range(PASSES):
+            nc.vector.tensor_copy(
+                out=wq_dealt[g][:].rearrange("p (r b i e) -> p b r i e", r=PACK, i=8, e=2),
+                in_=wq_raw[:, g, :].rearrange("p (b i r e) -> p b r i e", r=PACK, i=8, e=2),
+            )
+
+        interleave(nc.vector.tensor_copy, xq_bf[0], xq_raw[0], 0, XQ_ON_VECTOR)
+        interleave(nc.scalar.copy, xq_bf[0], xq_raw[0], XQ_ON_VECTOR, T)
+        deal_scales(wq_sc, wq_sc_raw)
+        quantize(xq_codes[0][:], xq_sc[0][:], xq_bf[0][:])
+        for r in range(PACK):
+            wq_pass(r, 0, True)
+
+        round_wc(nc.vector.tensor_copy, 0, 0)
+        round_wc(nc.scalar.copy, 0, 1)
+        deal_scales(wa_sc, wa_sc_raw)
+        quantize_wc(0, 0)
+        nc.vector.tensor_scalar(out=th_neg[:], in0=th_pos[:], scalar1=-1.0, scalar2=None, op0=ALU.mult)
+        quantize_wc(0, 1)
+        for r in range(PACK):
+            wc_pass(r, 0)
+
+        interleave(nc.vector.tensor_copy, xq_bf[1], xq_raw[1], 0, XQ_ON_VECTOR)
+        interleave(nc.scalar.copy, xq_bf[1], xq_raw[1], XQ_ON_VECTOR, T)
+        quantize(xq_codes[1][:], xq_sc[1][:], xq_bf[1][:])
+        for r in range(PACK):
+            wq_pass(r, 1, False)
+
+        round_wc(nc.vector.tensor_copy, 1, 0)
+        round_wc(nc.scalar.copy, 1, 1)
+        deal_wa(0)
+        quantize_wc(1, 0)
+        deal_wa(1)
+        quantize_wc(1, 1)
+
+        for r in range(PACK):
+            wc_pass(r, 1)
+            for g in range(PASSES):
+                wa_pass(r, g, g == PASSES - 1)
+            nc.scalar.activation(out=tanh_s[r][:], in_=s_acc[r][:], func=ACT.Tanh)
+        for r in (0, 1):
+            for h in range(2):
+                add_upper(r, h)
+            for h in range(2):
+                add_lower(r, h)
+        for h in range(2):
+            for r in (2, 3):
+                add_upper(r, h)
+            for r in (2, 3):
+                add_lower(r, h)
+            store_y(h)
+        interleave(nc.scalar.copy, y_bf[0], y[0], 0, HALF)
+        interleave(nc.vector.tensor_copy, y_bf[1], y[1], 0, LAST_ON_VECTOR)
+        interleave(nc.scalar.copy, y_bf[1], y[1], LAST_ON_VECTOR, HALF)
+        for h in range(2):
+            quantize(y_codes[h][:], y_sc[:, h * HALF : (h + 1) * HALF], y_bf[h][:])
+            store_words(h)
+        for quad in range(4):
+            queue = nc.scalar if quad % 2 else nc.sync
+            queue.dma_start(
+                out=out_2[0, 4 * quad : 4 * quad + 4, :].bitcast(I32),
+                in_=y_sc[32 * quad : 32 * quad + 4, :].bitcast(I32),
+            )

@@ -75,8 +75,8 @@ def tile_mix_sum_shrunk_by_threshold_pl_kernel(
                     in_=rows[4 * quad : 4 * quad + 4, :, :].bitcast(I32),
                 )
 
-        def load_rows(raw, src, g):
-            nc.sync.dma_start(
+        def load_rows(queue, raw, src, g):
+            queue.dma_start(
                 out=raw[:], in_=src[g * K_PASS : (g + 1) * K_PASS, :].rearrange("(p j) w -> p j w", j=PACK)
             )
 
@@ -149,10 +149,15 @@ def tile_mix_sum_shrunk_by_threshold_pl_kernel(
                 op0=ALU.min, op1=ALU.add,
             )
 
-        def store_y(h):
+        def store_y(h, lo, hi):
             nc.sync.dma_start(
-                out=out_0.rearrange("(p r) t -> p r t", r=PACK)[:, :, h * HALF : (h + 1) * HALF], in_=y[h][:]
+                out=out_0.rearrange("(p r) t -> p r t", r=PACK)[:, lo:hi, h * HALF : (h + 1) * HALF],
+                in_=y[h][:, lo:hi, :],
             )
+
+        def tanh_half(r, h):
+            cols = slice(h * HALF, (h + 1) * HALF)
+            nc.scalar.activation(out=tanh_s[r][:, cols], in_=s_acc[r][:, cols], func=ACT.Tanh)
 
         def store_words(h):
             nc.sync.dma_start(
@@ -175,14 +180,14 @@ def tile_mix_sum_shrunk_by_threshold_pl_kernel(
         nc.gpsimd.memset(xt_sc[:].rearrange("p g c -> p (g c)").bitcast(I32), 0)
         load_scales(nc.gpsimd, xt_sc, xt_scales)
         nc.sync.dma_start(out=wq_raw[:].bitcast(I32), in_=wq_words.rearrange("g p c -> p g c").bitcast(I32))
-        load_rows(xq_raw[0], xq, 0)
-        load_scales(nc.scalar, wq_sc_raw, wq_scales)
+        load_rows(nc.scalar, xq_raw[0], xq, 0)
+        load_scales(nc.sync, wq_sc_raw, wq_scales)
         nc.scalar.activation(out=warm_out[:], in_=warm_in[:], func=ACT.Tanh)
-        load_rows(wc_raw[0], wc, 0)
+        load_rows(nc.sync, wc_raw[0], wc, 0)
+        load_rows(nc.sync, xq_raw[1], xq, 1)
         nc.sync.dma_start(out=th_pos[:], in_=th.rearrange("(p r) o -> p (r o)", r=PACK))
         load_scales(nc.sync, wa_sc_raw, wa_scales)
-        load_rows(xq_raw[1], xq, 1)
-        load_rows(wc_raw[1], wc, 1)
+        load_rows(nc.sync, wc_raw[1], wc, 1)
         for g in range(PASSES):
             nc.sync.dma_start(out=wa_raw[g][:], in_=wa_words[g].rearrange("p n t -> p (n t)").bitcast(I32))
         for g in range(PASSES):
@@ -203,16 +208,16 @@ def tile_mix_sum_shrunk_by_threshold_pl_kernel(
 
         round_wc(nc.vector.tensor_copy, 0, 0)
         round_wc(nc.scalar.copy, 0, 1)
-        deal_scales(wa_sc, wa_sc_raw)
         quantize_wc(0, 0)
-        nc.vector.tensor_scalar(out=th_neg[:], in0=th_pos[:], scalar1=-1.0, scalar2=None, op0=ALU.mult)
         quantize_wc(0, 1)
         for r in range(PACK):
             wc_pass(r, 0)
 
         interleave(nc.vector.tensor_copy, xq_bf[1], xq_raw[1], 0, XQ_ON_VECTOR)
         interleave(nc.scalar.copy, xq_bf[1], xq_raw[1], XQ_ON_VECTOR, T)
+        deal_scales(wa_sc, wa_sc_raw)
         quantize(xq_codes[1][:], xq_sc[1][:], xq_bf[1][:])
+        nc.vector.tensor_scalar(out=th_neg[:], in0=th_pos[:], scalar1=-1.0, scalar2=None, op0=ALU.mult)
         for r in range(PACK):
             wq_pass(r, 1, False)
 
@@ -227,19 +232,30 @@ def tile_mix_sum_shrunk_by_threshold_pl_kernel(
             wc_pass(r, 1)
             for g in range(PASSES):
                 wa_pass(r, g, g == PASSES - 1)
-            nc.scalar.activation(out=tanh_s[r][:], in_=s_acc[r][:], func=ACT.Tanh)
         for r in (0, 1):
             for h in range(2):
-                add_upper(r, h)
-            for h in range(2):
-                add_lower(r, h)
+                tanh_half(r, h)
+        for h in range(2):
+            for r in (2, 3):
+                tanh_half(r, h)
+        for h in range(2):
+            add_upper(0, h)
+        for h in range(2):
+            add_lower(0, h)
+        for h in range(2):
+            add_upper(1, h)
+        add_lower(1, 0)
         for h in range(2):
             for r in (2, 3):
                 add_upper(r, h)
             for r in (2, 3):
                 add_lower(r, h)
-            store_y(h)
-        interleave(nc.scalar.copy, y_bf[0], y[0], 0, HALF)
+            if h == 0:
+                store_y(0, 0, PACK)
+                interleave(nc.scalar.copy, y_bf[0], y[0], 0, HALF)
+                add_lower(1, 1)
+                store_y(1, 0, 2)
+        store_y(1, 2, PACK)
         interleave(nc.vector.tensor_copy, y_bf[1], y[1], 0, LAST_ON_VECTOR)
         interleave(nc.scalar.copy, y_bf[1], y[1], LAST_ON_VECTOR, HALF)
         for h in range(2):

@@ -19,7 +19,7 @@ PACK = 4
 PASSES = 2
 K_PASS = P * PACK
 HALF = T // 2
-XQ_ON_VECTOR = 288
+XQ_ON_VECTOR = (192, 288)
 LAST_ON_VECTOR = 160
 
 
@@ -60,7 +60,7 @@ def tile_mix_sum_shrunk_by_threshold_pl_kernel(
         warm_out = new("warm_out", [P, 1], F32)
         tanh_s = [new("tanh_s%d" % r, [P, T], F32) for r in range(PACK)]
         upper = [[new("upper%d%d" % (r, h), [P, HALF], F32) for h in range(2)] for r in range(PACK)]
-        y = [new("y%d" % h, [P, PACK, HALF], F32) for h in range(2)]
+        y = new("y", [P, PACK, T], F32)
         y_bf = [new("y_bf%d" % h, [P, HALF * PACK], BF16) for h in range(2)]
         y_codes = [new("y_codes%d" % h, [P, HALF], I32) for h in range(2)]
         y_sc = new("y_sc", [P, T], U8)
@@ -69,20 +69,17 @@ def tile_mix_sum_shrunk_by_threshold_pl_kernel(
 
         def load_scales(queue, plane, scales):
             rows = scales.rearrange("g q c -> q g c")
-            for quad in range(4):
-                queue.dma_start(
-                    out=plane[32 * quad : 32 * quad + 4, :, :].bitcast(I32),
-                    in_=rows[4 * quad : 4 * quad + 4, :, :].bitcast(I32),
-                )
+            for i in range(4):
+                queue.dma_start(out=plane[i:P:32, :, :].bitcast(I32), in_=rows[i:16:4, :, :].bitcast(I32))
 
         def load_rows(queue, raw, src, g):
             queue.dma_start(
                 out=raw[:], in_=src[g * K_PASS : (g + 1) * K_PASS, :].rearrange("(p j) w -> p j w", j=PACK)
             )
 
-        def interleave(copy, bf, raw, lo, hi):
+        def interleave(copy, bf, raw, lo, hi, first=0):
             copy(
-                out=bf[:, PACK * lo : PACK * hi].rearrange("p (c i j) -> p c j i", i=4, j=PACK),
+                out=bf[:, PACK * (lo - first) : PACK * (hi - first)].rearrange("p (c i j) -> p c j i", i=4, j=PACK),
                 in_=raw[:, :, lo:hi].rearrange("p j (c i) -> p c j i", i=4),
             )
 
@@ -145,15 +142,12 @@ def tile_mix_sum_shrunk_by_threshold_pl_kernel(
         def add_lower(r, h):
             cols = slice(h * HALF, (h + 1) * HALF)
             nc.vector.scalar_tensor_tensor(
-                out=y[h][:, r, :], in0=p_acc[r][:, cols], scalar=th_neg[:, r : r + 1], in1=upper[r][h][:],
+                out=y[:, r, cols], in0=p_acc[r][:, cols], scalar=th_neg[:, r : r + 1], in1=upper[r][h][:],
                 op0=ALU.min, op1=ALU.add,
             )
 
-        def store_y(h, lo, hi):
-            nc.sync.dma_start(
-                out=out_0.rearrange("(p r) t -> p r t", r=PACK)[:, lo:hi, h * HALF : (h + 1) * HALF],
-                in_=y[h][:, lo:hi, :],
-            )
+        def store_y(rows, cols):
+            nc.sync.dma_start(out=out_0.rearrange("(p r) t -> p r t", r=PACK)[:, rows, cols], in_=y[:, rows, cols])
 
         def tanh_half(r, h):
             cols = slice(h * HALF, (h + 1) * HALF)
@@ -181,11 +175,11 @@ def tile_mix_sum_shrunk_by_threshold_pl_kernel(
         load_scales(nc.gpsimd, xt_sc, xt_scales)
         nc.sync.dma_start(out=wq_raw[:].bitcast(I32), in_=wq_words.rearrange("g p c -> p g c").bitcast(I32))
         load_rows(nc.scalar, xq_raw[0], xq, 0)
+        nc.scalar.dma_start(out=th_pos[:], in_=th.rearrange("(p r) o -> p (r o)", r=PACK))
         load_scales(nc.sync, wq_sc_raw, wq_scales)
         nc.scalar.activation(out=warm_out[:], in_=warm_in[:], func=ACT.Tanh)
-        load_rows(nc.sync, wc_raw[0], wc, 0)
         load_rows(nc.sync, xq_raw[1], xq, 1)
-        nc.sync.dma_start(out=th_pos[:], in_=th.rearrange("(p r) o -> p (r o)", r=PACK))
+        load_rows(nc.sync, wc_raw[0], wc, 0)
         load_scales(nc.sync, wa_sc_raw, wa_scales)
         load_rows(nc.sync, wc_raw[1], wc, 1)
         for g in range(PASSES):
@@ -199,27 +193,27 @@ def tile_mix_sum_shrunk_by_threshold_pl_kernel(
                 in_=wq_raw[:, g, :].rearrange("p (b i r e) -> p b r i e", r=PACK, i=8, e=2),
             )
 
-        interleave(nc.vector.tensor_copy, xq_bf[0], xq_raw[0], 0, XQ_ON_VECTOR)
-        interleave(nc.scalar.copy, xq_bf[0], xq_raw[0], XQ_ON_VECTOR, T)
+        interleave(nc.vector.tensor_copy, xq_bf[0], xq_raw[0], 0, XQ_ON_VECTOR[0])
+        interleave(nc.scalar.copy, xq_bf[0], xq_raw[0], XQ_ON_VECTOR[0], T)
         deal_scales(wq_sc, wq_sc_raw)
         quantize(xq_codes[0][:], xq_sc[0][:], xq_bf[0][:])
         for r in range(PACK):
             wq_pass(r, 0, True)
 
+        interleave(nc.vector.tensor_copy, xq_bf[1], xq_raw[1], 0, XQ_ON_VECTOR[1])
+        interleave(nc.scalar.copy, xq_bf[1], xq_raw[1], XQ_ON_VECTOR[1], T)
+        quantize(xq_codes[1][:], xq_sc[1][:], xq_bf[1][:])
+        for r in range(PACK):
+            wq_pass(r, 1, False)
+
         round_wc(nc.vector.tensor_copy, 0, 0)
         round_wc(nc.scalar.copy, 0, 1)
+        deal_scales(wa_sc, wa_sc_raw)
         quantize_wc(0, 0)
+        nc.vector.tensor_scalar(out=th_neg[:], in0=th_pos[:], scalar1=-1.0, scalar2=None, op0=ALU.mult)
         quantize_wc(0, 1)
         for r in range(PACK):
             wc_pass(r, 0)
-
-        interleave(nc.vector.tensor_copy, xq_bf[1], xq_raw[1], 0, XQ_ON_VECTOR)
-        interleave(nc.scalar.copy, xq_bf[1], xq_raw[1], XQ_ON_VECTOR, T)
-        deal_scales(wa_sc, wa_sc_raw)
-        quantize(xq_codes[1][:], xq_sc[1][:], xq_bf[1][:])
-        nc.vector.tensor_scalar(out=th_neg[:], in0=th_pos[:], scalar1=-1.0, scalar2=None, op0=ALU.mult)
-        for r in range(PACK):
-            wq_pass(r, 1, False)
 
         round_wc(nc.vector.tensor_copy, 1, 0)
         round_wc(nc.scalar.copy, 1, 1)
@@ -238,26 +232,22 @@ def tile_mix_sum_shrunk_by_threshold_pl_kernel(
         for h in range(2):
             for r in (2, 3):
                 tanh_half(r, h)
-        for h in range(2):
-            add_upper(0, h)
-        for h in range(2):
-            add_lower(0, h)
-        for h in range(2):
-            add_upper(1, h)
-        add_lower(1, 0)
+        for r in (0, 1):
+            for h in range(2):
+                add_upper(r, h)
+            for h in range(2):
+                add_lower(r, h)
+            store_y(slice(r, r + 1), slice(0, T))
         for h in range(2):
             for r in (2, 3):
                 add_upper(r, h)
             for r in (2, 3):
                 add_lower(r, h)
+            store_y(slice(2, PACK), slice(h * HALF, (h + 1) * HALF))
             if h == 0:
-                store_y(0, 0, PACK)
-                interleave(nc.scalar.copy, y_bf[0], y[0], 0, HALF)
-                add_lower(1, 1)
-                store_y(1, 0, 2)
-        store_y(1, 2, PACK)
-        interleave(nc.vector.tensor_copy, y_bf[1], y[1], 0, LAST_ON_VECTOR)
-        interleave(nc.scalar.copy, y_bf[1], y[1], LAST_ON_VECTOR, HALF)
+                interleave(nc.scalar.copy, y_bf[0], y, 0, HALF)
+        interleave(nc.vector.tensor_copy, y_bf[1], y, HALF, HALF + LAST_ON_VECTOR, HALF)
+        interleave(nc.scalar.copy, y_bf[1], y, HALF + LAST_ON_VECTOR, T, HALF)
         for h in range(2):
             quantize(y_codes[h][:], y_sc[:, h * HALF : (h + 1) * HALF], y_bf[h][:])
             store_words(h)

from contextlib import ExitStack

import concourse.mybir as mybir

K, L, T, N = 1024, 1024, 512, 512
FLOPS = 2 * (K + 2 * L) * T * N

F32 = mybir.dt.float32
BF16 = mybir.dt.bfloat16
I32 = mybir.dt.int32
U8 = mybir.dt.uint8
FP8X4 = mybir.dt.float8_e4m3fn_x4
FP4X4 = mybir.dt.float4_e2m1fn_x4
ALU = mybir.AluOpType
ACT = mybir.ActivationFunctionType

P = 128
PACK = 4
PASSES = 2
K_PASS = P * PACK
HALF = T // 2
XQ_ON_VECTOR = (192, 288)
LAST_ON_VECTOR = 160


def tile_mix_sum_shrunk_by_threshold_pl_kernel(
    tc, xt_words, xt_scales, wa_words, wa_scales, xq, wq_words, wq_scales, wc, th, out_0, out_1, out_2
):
    nc = tc.nc

    with ExitStack() as ctx:
        sb = ctx.enter_context(tc.tile_pool(name="sb", bufs=1))
        ps = ctx.enter_context(tc.psum_pool(name="ps", bufs=1))
        ctx.enter_context(tc.manual_schedule())

        def new(name, shape, dtype):
            return sb.tile(shape, dtype, name=name, align_bytes=64)

        wq_raw = new("wq_raw", [P, PASSES, 2 * N], U8)
        wq_dealt = [new("wq_dealt%d" % g, [P, 2 * N], U8) for g in range(PASSES)]
        wa_raw = [new("wa_raw%d" % g, [P, N], I32) for g in range(PASSES)]
        wa_dealt = [new("wa_dealt%d" % g, [P, N], I32) for g in range(PASSES)]
        xt_codes = [new("xt_codes%d" % g, [P, 2 * T], U8) for g in range(PASSES)]
        wq_sc_raw = new("wq_sc_raw", [P, PASSES, N], U8)
        wa_sc_raw = new("wa_sc_raw", [P, PASSES, N], U8)
        wq_sc = new("wq_sc", [P, PASSES, N], U8)
        wa_sc = new("wa_sc", [P, PASSES, N], U8)
        xt_sc = new("xt_sc", [P, PASSES, T], U8)
        xq_raw = [new("xq_raw%d" % g, [P, PACK, T], F32) for g in range(PASSES)]
        wc_raw = [new("wc_raw%d" % g, [P, PACK, N], F32) for g in range(PASSES)]
        xq_bf = [new("xq_bf%d" % g, [P, T * PACK], BF16) for g in range(PASSES)]
        xq_codes = [new("xq_codes%d" % g, [P, T], I32) for g in range(PASSES)]
        xq_sc = [new("xq_sc%d" % g, [P, T], U8) for g in range(PASSES)]
        wc_bf = [[new("wc_bf%d%d" % (g, h), [P, 2 * P * PACK], BF16) for h in range(2)] for g in range(PASSES)]
        wc_codes = [[new("wc_codes%d%d" % (g, h), [P, 2 * P], I32) for h in range(2)] for g in range(PASSES)]
        wc_sc = [[new("wc_sc%d%d" % (g, h), [P, 2 * P], U8) for h in range(2)] for g in range(PASSES)]
        th_pos = new("th_pos", [P, PACK], F32)
        th_neg = new("th_neg", [P, PACK], F32)
        warm_in = new("warm_in", [P, 1], F32)
        warm_out = new("warm_out", [P, 1], F32)
        tanh_s = [new("tanh_s%d" % r, [P, T], F32) for r in range(PACK)]
        upper = [[new("upper%d%d" % (r, h), [P, HALF], F32) for h in range(2)] for r in range(PACK)]
        y = new("y", [P, PACK, T], F32)
        y_bf = [new("y_bf%d" % h, [P, HALF * PACK], BF16) for h in range(2)]
        y_codes = [new("y_codes%d" % h, [P, HALF], I32) for h in range(2)]
        y_sc = new("y_sc", [P, T], U8)
        p_acc = [ps.tile([P, T], F32, name="p_acc%d" % r) for r in range(PACK)]
        s_acc = [ps.tile([P, T], F32, name="s_acc%d" % r) for r in range(PACK)]

        def load_scales(queue, plane, scales):
            rows = scales.rearrange("g q c -> q g c")
            for i in range(4):
                queue.dma_start(out=plane[i:P:32, :, :].bitcast(I32), in_=rows[i:16:4, :, :].bitcast(I32))

        def load_rows(queue, raw, src, g):
            queue.dma_start(
                out=raw[:], in_=src[g * K_PASS : (g + 1) * K_PASS, :].rearrange("(p j) w -> p j w", j=PACK)
            )

        def interleave(copy, bf, raw, lo, hi, first=0):
            copy(
                out=bf[:, PACK * (lo - first) : PACK * (hi - first)].rearrange("p (c i j) -> p c j i", i=4, j=PACK),
                in_=raw[:, :, lo:hi].rearrange("p j (c i) -> p c j i", i=4),
            )

        def round_wc(copy, g, h):
            copy(
                out=wc_bf[g][h][:].rearrange("p (r m j) -> p m r j", r=2, j=PACK),
                in_=wc_raw[g][:].rearrange("p j (m r) -> p m r j", r=PACK)[:, :, 2 * h : 2 * h + 2, :],
            )

        def quantize(codes, scales, bf):
            nc.vector.quantize_mx(out=codes.bitcast(FP8X4), scales=scales, in_=bf)

        def deal_scales(dealt, raw):
            nc.vector.tensor_copy(
                out=dealt[:].rearrange("p g (r b i) -> p g b r i", r=PACK, i=16),
                in_=raw[:].rearrange("p g (b i r) -> p g b r i", r=PACK, i=16),
            )

        def wq_pass(r, g, start):
            nc.tensor.matmul_mx(
                out=p_acc[r][:],
                lhsT=wq_dealt[g][:, 2 * P * r : 2 * P * (r + 1)].bitcast(FP4X4),
                lhsT_scale=wq_sc[:, g, P * r : P * (r + 1)],
                rhs=xq_codes[g][:].bitcast(FP8X4),
                rhs_scale=xq_sc[g][:],
                start=start,
                stop=False,
            )

        def wa_pass(r, g, stop):
            nc.tensor.matmul_mx(
                out=p_acc[r][:],
                lhsT=wa_dealt[g][:, P * r : P * (r + 1)].bitcast(FP8X4),
                lhsT_scale=wa_sc[:, g, P * r : P * (r + 1)],
                rhs=xt_codes[g][:].bitcast(FP4X4),
                rhs_scale=xt_sc[:, g, :],
                start=False,
                stop=stop,
            )

        def wc_pass(r, g):
            cols = slice(P * (r % 2), P * (r % 2 + 1))
            nc.tensor.matmul_mx(
                out=s_acc[r][:],
                lhsT=wc_codes[g][r // 2][:, cols].bitcast(FP8X4),
                lhsT_scale=wc_sc[g][r // 2][:, cols],
                rhs=xq_codes[g][:].bitcast(FP8X4),
                rhs_scale=xq_sc[g][:],
                start=(g == 0),
                stop=(g == PASSES - 1),
            )

        def add_upper(r, h):
            cols = slice(h * HALF, (h + 1) * HALF)
            nc.vector.scalar_tensor_tensor(
                out=upper[r][h][:], in0=p_acc[r][:, cols], scalar=th_pos[:, r : r + 1], in1=tanh_s[r][:, cols],
                op0=ALU.max, op1=ALU.add,
            )

        def add_lower(r, h):
            cols = slice(h * HALF, (h + 1) * HALF)
            nc.vector.scalar_tensor_tensor(
                out=y[:, r, cols], in0=p_acc[r][:, cols], scalar=th_neg[:, r : r + 1], in1=upper[r][h][:],
                op0=ALU.min, op1=ALU.add,
            )

        def store_y(rows, cols):
            nc.sync.dma_start(out=out_0.rearrange("(p r) t -> p r t", r=PACK)[:, rows, cols], in_=y[:, rows, cols])

        def tanh_half(r, h):
            cols = slice(h * HALF, (h + 1) * HALF)
            nc.scalar.activation(out=tanh_s[r][:, cols], in_=s_acc[r][:, cols], func=ACT.Tanh)

        def store_words(h):
            nc.sync.dma_start(
                out=out_1[0].rearrange("p c r -> p (c r)").bitcast(I32)[:, h * HALF : (h + 1) * HALF],
                in_=y_codes[h][:],
            )

        def deal_wa(g):
            nc.vector.tensor_copy(
                out=wa_dealt[g][:].rearrange("p (r b i) -> p b r i", r=PACK, i=4),
                in_=wa_raw[g][:].rearrange("p (b i r) -> p b r i", r=PACK, i=4),
            )

        def quantize_wc(g, h):
            quantize(wc_codes[g][h][:], wc_sc[g][h][:], wc_bf[g][h][:])

        for plane in (wq_sc_raw, wa_sc_raw):
            nc.vector.memset(plane[:].rearrange("p g c -> p (g c)").bitcast(I32), 0)
        nc.vector.memset(warm_in[:], 0.0)
        nc.gpsimd.memset(xt_sc[:].rearrange("p g c -> p (g c)").bitcast(I32), 0)
        load_scales(nc.gpsimd, xt_sc, xt_scales)
        nc.sync.dma_start(out=wq_raw[:].bitcast(I32), in_=wq_words.rearrange("g p c -> p g c").bitcast(I32))
        load_rows(nc.scalar, xq_raw[0], xq, 0)
        nc.scalar.dma_start(out=th_pos[:], in_=th.rearrange("(p r) o -> p (r o)", r=PACK))
        load_scales(nc.sync, wq_sc_raw, wq_scales)
        nc.scalar.activation(out=warm_out[:], in_=warm_in[:], func=ACT.Tanh)
        load_rows(nc.sync, xq_raw[1], xq, 1)
        load_rows(nc.sync, wc_raw[0], wc, 0)
        load_scales(nc.sync, wa_sc_raw, wa_scales)
        load_rows(nc.sync, wc_raw[1], wc, 1)
        for g in range(PASSES):
            nc.sync.dma_start(out=wa_raw[g][:], in_=wa_words[g].rearrange("p n t -> p (n t)").bitcast(I32))
        for g in range(PASSES):
            nc.sync.dma_start(out=xt_codes[g][:].bitcast(I32), in_=xt_words[g].bitcast(I32))

        for g in range(PASSES):
            nc.vector.tensor_copy(
                out=wq_dealt[g][:].rearrange("p (r b i e) -> p b r i e", r=PACK, i=8, e=2),
                in_=wq_raw[:, g, :].rearrange("p (b i r e) -> p b r i e", r=PACK, i=8, e=2),
            )

        interleave(nc.vector.tensor_copy, xq_bf[0], xq_raw[0], 0, XQ_ON_VECTOR[0])
        interleave(nc.scalar.copy, xq_bf[0], xq_raw[0], XQ_ON_VECTOR[0], T)
        deal_scales(wq_sc, wq_sc_raw)
        quantize(xq_codes[0][:], xq_sc[0][:], xq_bf[0][:])
        for r in range(PACK):
            wq_pass(r, 0, True)

        interleave(nc.vector.tensor_copy, xq_bf[1], xq_raw[1], 0, XQ_ON_VECTOR[1])
        interleave(nc.scalar.copy, xq_bf[1], xq_raw[1], XQ_ON_VECTOR[1], T)
        quantize(xq_codes[1][:], xq_sc[1][:], xq_bf[1][:])
        for r in range(PACK):
            wq_pass(r, 1, False)

        round_wc(nc.vector.tensor_copy, 0, 0)
        round_wc(nc.scalar.copy, 0, 1)
        deal_scales(wa_sc, wa_sc_raw)
        quantize_wc(0, 0)
        nc.vector.tensor_scalar(out=th_neg[:], in0=th_pos[:], scalar1=-1.0, scalar2=None, op0=ALU.mult)
        quantize_wc(0, 1)
        for r in range(PACK):
            wc_pass(r, 0)

        round_wc(nc.vector.tensor_copy, 1, 0)
        round_wc(nc.scalar.copy, 1, 1)
        deal_wa(0)
        quantize_wc(1, 0)
        deal_wa(1)
        quantize_wc(1, 1)

        for r in range(PACK):
            wc_pass(r, 1)
            for g in range(PASSES):
                wa_pass(r, g, g == PASSES - 1)
        for r in (0, 1):
            for h in range(2):
                tanh_half(r, h)
        for h in range(2):
            for r in (2, 3):
                tanh_half(r, h)
        for r in (0, 1):
            for h in range(2):
                add_upper(r, h)
            for h in range(2):
                add_lower(r, h)
            store_y(slice(r, r + 1), slice(0, T))
        for h in range(2):
            for r in (2, 3):
                add_upper(r, h)
            for r in (2, 3):
                add_lower(r, h)
            store_y(slice(2, PACK), slice(h * HALF, (h + 1) * HALF))
            if h == 0:
                interleave(nc.scalar.copy, y_bf[0], y, 0, HALF)
        interleave(nc.vector.tensor_copy, y_bf[1], y, HALF, HALF + LAST_ON_VECTOR, HALF)
        interleave(nc.scalar.copy, y_bf[1], y, HALF + LAST_ON_VECTOR, T, HALF)
        for h in range(2):
            quantize(y_codes[h][:], y_sc[:, h * HALF : (h + 1) * HALF], y_bf[h][:])
            store_words(h)
        for quad in range(4):
            queue = nc.scalar if quad % 2 else nc.sync
            queue.dma_start(
                out=out_2[0, 4 * quad : 4 * quad + 4, :].bitcast(I32),
                in_=y_sc[32 * quad : 32 * quad + 4, :].bitcast(I32),
            )
